import numpy as np
import ml_dtypes


def mxq(x, axis, fmt="e4m3"):
    dtype, down = {"e4m3": (ml_dtypes.float8_e4m3fn, 7), "e5m2": (ml_dtypes.float8_e5m2, 14)}[fmt]
    v = np.moveaxis(np.asarray(x, np.float32).astype(ml_dtypes.bfloat16).astype(np.float64), axis, -1)
    blocks = v.reshape(v.shape[:-1] + (-1, 32))
    amax = np.abs(blocks).max(-1, keepdims=True)
    byte = np.maximum(np.where(amax > 0, np.frexp(amax)[1] - 1 + 127, 0) - down, 1)
    scale = np.exp2(byte - 127.0)
    codes = (blocks / scale).astype(np.float32).astype(dtype).astype(np.float64)
    return np.moveaxis((codes * scale).reshape(v.shape), -1, axis)


WIDE = False


def mx_kscale(k):
    if not WIDE:
        return np.ones(k)
    levels = np.array([18, -18])
    if k % 512:
        return np.exp2(np.random.permutation(np.resize(levels, k // 32))).repeat(32)
    a = np.empty((k // 512, 16))
    for p in range(k // 512):
        a[p, :8] = np.random.permutation(np.resize(levels, 8))
        for g in range(8):
            far = levels[np.abs(levels - a[p, g]) >= 10]
            a[p, g + 8] = far[np.random.randint(len(far))]
    return np.exp2(a.ravel()).repeat(32)


def f64(x):
    return np.asarray(x).astype(np.float64)


def striped(idx):
    return np.tile(np.asarray(idx).reshape(-1, 16).T, (8, 1)).astype(np.uint16)


def unstriped(offs):
    return offs[:16].T.reshape(-1).astype(np.int64)

def planes(y):
    n, m = y.shape
    v = y.astype(np.float32).astype(ml_dtypes.bfloat16).astype(np.float64).reshape(n // 32, 32, m)
    top = np.abs(v).max(1)
    byte = np.clip(np.where(top > 0, np.frexp(top)[1] - 1 + 127 - 7, 1), 1, 254)
    codes = (v * np.exp2(127.0 - byte)[:, None, :]).reshape(n, m).astype(np.float32).astype(ml_dtypes.float8_e4m3fn).view(np.uint8)
    words = codes.reshape(n // 512, 128, 4, m).transpose(0, 1, 3, 2)
    return np.ascontiguousarray(words), np.ascontiguousarray(byte.astype(np.uint8).reshape(n // 512, 16, m))


B, N, T, D, R = 1, 512, 2048, 512, 512


def setup_inputs():
    n = np.random.standard_normal
    idx = np.random.permutation(T)[:B * N]
    s = mx_kscale(D)[:, None]
    z = mx_kscale(R)[:, None]
    q = n((B, D, R))
    do = n((B, D, R))
    return {
        "qT": (q * s).astype(np.float32),
        "cT": (n((D, T)) * (0.50 / np.sqrt(D)) / s).astype(np.float32),
        "doT": (do * s).astype(np.float32),
        "lse": (np.log(N) + 0.12 + 0.1 * n((B, R, 1))).astype(np.float32),
        "delta": (0.3 * n((B, R, 1))).astype(np.float32),
        "rw": (np.random.uniform(0.5, 1.5, (B, R, 1)) * N / np.sqrt(R) * z).astype(np.float32),
        "qm": (q.transpose(0, 2, 1) / z).astype(np.float32),
        "dom": (do.transpose(0, 2, 1) / z).astype(np.float32),
        "offs": striped(idx),
    }


def reference(qT, cT, doT, lse, delta, rw, qm, dom, offs):
    idx = unstriped(offs)
    pick = lambda x: x[:, idx].reshape(x.shape[0], B, N).transpose(1, 0, 2)
    cq = mxq(pick(f64(cT)), 1, "e4m3")
    a = mxq(f64(qT), 1, "e4m3").transpose(0, 2, 1) @ cq
    p = np.exp(a - f64(lse))
    dp = mxq(f64(doT), 1, "e5m2").transpose(0, 2, 1) @ cq
    ds = f64(rw) * p * (dp - f64(delta))
    dk = mxq(f64(qm), 1, "e4m3").transpose(0, 2, 1) @ mxq(ds, 1, "e5m2")
    dv = mxq(f64(dom), 1, "e5m2").transpose(0, 2, 1) @ mxq(f64(rw) * p, 1, "e4m3")
    gc = np.zeros((D, T))
    gc[:, idx] = (dk + dv).transpose(1, 0, 2).reshape(D, B * N)
    out_0 = gc
    return (out_0,) + planes(out_0)

@@ -1,0 +1,184 @@
+from contextlib import ExitStack
+
+import concourse.mybir as mybir
+
+N, T, D, R = 512, 2048, 512, 512
+FLOPS = 4 * 2 * 512 * 512 * 512
+
+F32 = mybir.dt.float32
+BF16 = mybir.dt.bfloat16
+I32 = mybir.dt.int32
+U32 = mybir.dt.uint32
+U16 = mybir.dt.uint16
+U8 = mybir.dt.uint8
+E4 = mybir.dt.float8_e4m3fn_x4
+E5 = mybir.dt.float8_e5m2_x4
+ALU = mybir.AluOpType
+ACT = mybir.ActivationFunctionType
+
+P = 128
+LANES = 4
+CHUNK = 512
+HALF = N // 2
+
+
+def tile_attend_gat_pl_lse_c_kernel(
+    tc, qT, cT, doT, lse, delta, rw, qm, dom, offs, out_0, out_1, out_2
+):
+    nc = tc.nc
+    with ExitStack() as ctx:
+        keep = ctx.enter_context(tc.tile_pool(name="keep", bufs=1))
+        psum = ctx.enter_context(tc.psum_pool(name="psum", bufs=1))
+
+        def copy(engine, out, in_):
+            if engine == "scalar":
+                nc.scalar.copy(out, in_)
+            else:
+                nc.vector.tensor_copy(out, in_)
+
+        def load_rows(name, src):
+            raw = keep.tile([P, LANES, 512], F32, name=name)
+            nc.sync.dma_start(raw[:], src[0].rearrange("(p l) c -> p l c", l=LANES))
+            return raw
+
+        def load_column(name, src):
+            col = keep.tile([P, LANES], F32, name=name)
+            nc.scalar.dma_start(col[:], src[0].rearrange("(p l) o -> p (l o)", l=LANES))
+            return col
+
+        def deal(name, raw, shares):
+            grouped = keep.tile([P, LANES, P, LANES], BF16, name=name, align_bytes=64)
+            dst = grouped[:].rearrange("p j m l -> p m l j")
+            src = raw[:].rearrange("p l (m j) -> p m l j", j=LANES)
+            for engine, m0, m1 in shares:
+                copy(engine, dst[:, m0:m1], src[:, m0:m1])
+            return grouped[:].rearrange("p j m l -> p (j m l)")
+
+        def weave(name, planes, shares):
+            width = planes.shape[2]
+            grouped = keep.tile([P, width, LANES], BF16, name=name, align_bytes=64)
+            dst = grouped[:].rearrange("p (c i) l -> p c l i", i=4)
+            src = planes.rearrange("p l (c i) -> p c l i", i=4)
+            for engine, c0, c1 in shares:
+                copy(engine, dst[:, c0:c1], src[:, c0:c1])
+            return grouped[:].rearrange("p n l -> p (n l)")
+
+        def quantize(name, grouped, fmt):
+            codes = keep.tile([P, 512], U32, name=name + "_codes", align_bytes=64)
+            scales = keep.tile([P, 512], U8, name=name + "_scales", align_bytes=64)
+            nc.vector.quantize_mx(out=codes[:].bitcast(fmt), scales=scales[:], in_=grouped)
+            return codes, scales, fmt
+
+        def product(bank, stationary, j, moving, start, stop):
+            cols = slice(P * j, P * (j + 1))
+            nc.tensor.matmul_mx(
+                out=bank[:],
+                lhsT=stationary[0][:, cols].bitcast(stationary[2]),
+                lhsT_scale=stationary[1][:, cols],
+                rhs=moving[0][:].bitcast(moving[2]),
+                rhs_scale=moving[1][:],
+                start=start,
+                stop=stop,
+            )
+
+        offsets = keep.tile([P, N // 16], U16, name="offsets")
+        c_planes = cT.rearrange("(p l) t -> l p t", l=LANES)
+        pool = [keep.tile([P, T], F32, name="pool%d" % l) for l in range(LANES)]
+        nc.sync.dma_start(pool[0][:], c_planes[0])
+        nc.sync.dma_start(offsets[:], offs)
+        for l in range(1, LANES):
+            nc.sync.dma_start(pool[l][:], c_planes[l])
+        lse_sb = load_column("lse_sb", lse)
+        delta_sb = load_column("delta_sb", delta)
+        rw_sb = load_column("rw_sb", rw)
+        q_raw = load_rows("q_raw", qT)
+        do_raw = load_rows("do_raw", doT)
+        dom_raw = load_rows("dom_raw", dom)
+        qm_raw = load_rows("qm_raw", qm)
+
+        windows = [keep.tile([P, T], F32, name="window%d" % j) for j in range(LANES)]
+        for j in range(LANES):
+            (nc.vector if j < 2 else nc.gpsimd).memset(windows[j][:], 0.0)
+
+        neg_lse = keep.tile([P, LANES], F32, name="neg_lse")
+        nc.scalar.activation(neg_lse[:], lse_sb[:], ACT.Copy, scale=-1.0)
+
+        c_grouped = keep.tile([P, N, LANES], BF16, name="c_grouped", align_bytes=64)
+        for l in range(LANES):
+            nc.vector.tensor_copy(c_grouped[:, :, l], pool[l][:].indirect(offsets[:]))
+        c_mx = quantize("c", c_grouped[:].rearrange("p n l -> p (n l)"), E4)
+
+        q_mx = quantize("q", deal("q_grouped", q_raw, [("vector", 0, 88), ("scalar", 88, P)]), E4)
+        a_banks = [psum.tile([P, N], F32, name="bank%d" % r) for r in range(LANES)]
+        p_sb = keep.tile([P, LANES, N], F32, name="p_sb")
+        for r in range(LANES):
+            product(a_banks[r], q_mx, r, c_mx, True, True)
+        for r in range(LANES):
+            nc.scalar.activation(p_sb[:, r, :], a_banks[r][:], ACT.Exp, bias=neg_lse[:, r : r + 1], scale=1.0)
+
+        do_mx = quantize("do", deal("do_grouped", do_raw, [("vector", 0, P)]), E5)
+        dp_banks = [psum.tile([P, N], F32, name="bank%d" % (LANES + r)) for r in range(LANES)]
+        for r in range(LANES):
+            product(dp_banks[r], do_mx, r, c_mx, True, True)
+
+        pw_sb = keep.tile([P, LANES, N], F32, name="pw_sb")
+        ds_sb = keep.tile([P, LANES, N], F32, name="ds_sb")
+        for r in range(LANES):
+            nc.vector.tensor_scalar(pw_sb[:, r, :], p_sb[:, r, :], rw_sb[:, r : r + 1], None, ALU.mult)
+        dom_grouped = deal("dom_grouped", dom_raw, [("scalar", 0, P)])
+        for r in range(LANES):
+            nc.vector.scalar_tensor_tensor(
+                ds_sb[:, r, :], dp_banks[r][:], delta_sb[:, r : r + 1], pw_sb[:, r, :], ALU.subtract, ALU.mult
+            )
+        pw_grouped = weave("pw_grouped", pw_sb[:], [("vector", 0, P)])
+        dom_mx = quantize("dom", dom_grouped, E5)
+        qm_grouped = deal("qm_grouped", qm_raw, [("scalar", 0, P)])
+        pw_mx = quantize("pw", pw_grouped, E4)
+        ds_grouped = weave("ds_grouped", ds_sb[:], [("vector", 0, 64), ("scalar", 64, P)])
+        qm_mx = quantize("qm", qm_grouped, E4)
+        ds_mx = quantize("ds", ds_grouped, E5)
+
+        g_banks = [psum.tile([P, N], F32, name="bank%d" % j) for j in range(LANES)]
+        for j in range(LANES):
+            product(g_banks[j], dom_mx, j, pw_mx, True, False)
+        for j in range(LANES):
+            product(g_banks[j], qm_mx, j, ds_mx, False, True)
+
+        out_planes = out_0.rearrange("(p l) t -> l p t", l=LANES)
+        for j in range(LANES):
+            g_sb = keep.tile([P, N], F32, name="g_sb%d" % j)
+            if j % 2 == 0:
+                nc.scalar.copy(g_sb[:], g_banks[j][:])
+                for h in range(2):
+                    nc.scalar.activation(
+                        windows[j][:].indirect(offsets[:, 16 * h : 16 * (h + 1)]),
+                        g_sb[:, HALF * h : HALF * (h + 1)],
+                        ACT.Copy,
+                    )
+            else:
+                nc.vector.tensor_copy(g_sb[:], g_banks[j][:])
+                nc.vector.tensor_copy(windows[j][:].indirect(offsets[:]), g_sb[:])
+            nc.sync.dma_start(out_planes[j], windows[j][:])
+
+        chunks = T // CHUNK
+        words = out_1.rearrange("o p t b -> p (o t b)").bitcast(I32)
+        y_scales = keep.tile([P, CHUNK], U8, name="y_scales", align_bytes=64)
+        rounded = [keep.tile([P, LANES, CHUNK], BF16, name="rounded%d" % u) for u in range(chunks)]
+        for u in range(chunks):
+            cols = slice(CHUNK * u, CHUNK * (u + 1))
+            for j in range(LANES):
+                copy("scalar" if j < 2 else "vector", rounded[u][:, j, :], windows[j][:, cols])
+        for u in range(chunks):
+            cols = slice(CHUNK * u, CHUNK * (u + 1))
+            shares = [[("vector", 0, P)], [("vector", 0, P)], [("vector", 0, 80), ("scalar", 80, P)], [("scalar", 0, P)]][u]
+            y_grouped = weave("y_grouped%d" % u, rounded[u][:], shares)
+            y_codes = keep.tile([P, CHUNK], U32, name="y_codes%d" % u, align_bytes=64)
+            nc.vector.quantize_mx(out=y_codes[:].bitcast(E4), scales=y_scales[LANES * u :, :], in_=y_grouped)
+            nc.sync.dma_start(words[:, cols], y_codes[:].bitcast(I32))
+        scale_rows = out_2[0].bitcast(I32).rearrange("f (u c) -> u f c", u=chunks)
+        for quad in range(4):
+            queue = nc.sync if quad % 2 == 0 else nc.scalar
+            queue.dma_start(
+                scale_rows[:, 4 * quad : 4 * quad + 4, :],
+                y_scales[32 * quad : 32 * quad + 16, :].bitcast(I32),
+            )

@@ -46,13 +46,12 @@ def tile_attend_gat_pl_lse_c_kernel(
             nc.scalar.dma_start(col[:], src[0].rearrange("(p l) o -> p (l o)", l=LANES))
             return col
 
-        def deal(name, raw, shares):
-            grouped = keep.tile([P, LANES, P, LANES], BF16, name=name, align_bytes=64)
-            dst = grouped[:].rearrange("p j m l -> p m l j")
-            src = raw[:].rearrange("p l (m j) -> p m l j", j=LANES)
-            for engine, m0, m1 in shares:
-                copy(engine, dst[:, m0:m1], src[:, m0:m1])
-            return grouped[:].rearrange("p j m l -> p (j m l)")
+        def deal(engine, dst, raw, half):
+            src = raw[:].rearrange("p l (m h j) -> p h m l j", h=2, j=2)[:, half]
+            copy(engine, dst.rearrange("p (j m l) -> p m l j", j=2, l=LANES), src)
+
+        def grouped_tile(name, words):
+            return keep.tile([P, words * LANES], BF16, name=name, align_bytes=64)
 
         def weave(name, planes, shares):
             width = planes.shape[2]
@@ -64,8 +63,9 @@ def tile_attend_gat_pl_lse_c_kernel(
             return grouped[:].rearrange("p n l -> p (n l)")
 
         def quantize(name, grouped, fmt):
-            codes = keep.tile([P, 512], U32, name=name + "_codes", align_bytes=64)
-            scales = keep.tile([P, 512], U8, name=name + "_scales", align_bytes=64)
+            words = grouped.shape[1] // LANES
+            codes = keep.tile([P, words], U32, name=name + "_codes", align_bytes=64)
+            scales = keep.tile([P, words], U8, name=name + "_scales", align_bytes=64)
             nc.vector.quantize_mx(out=codes[:].bitcast(fmt), scales=scales[:], in_=grouped)
             return codes, scales, fmt
 
@@ -97,8 +97,11 @@ def tile_attend_gat_pl_lse_c_kernel(
         qm_raw = load_rows("qm_raw", qm)
 
         windows = [keep.tile([P, T], F32, name="window%d" % j) for j in range(LANES)]
-        for j in range(LANES):
-            (nc.vector if j < 2 else nc.gpsimd).memset(windows[j][:], 0.0)
+        for j in range(2):
+            nc.vector.memset(windows[j][:], 0.0)
+        for j in range(2, LANES):
+            for h in range(2):
+                nc.gpsimd.memset(windows[j][:, h * T // 2 : (h + 1) * T // 2], 0.0)
 
         neg_lse = keep.tile([P, LANES], F32, name="neg_lse")
         nc.scalar.activation(neg_lse[:], lse_sb[:], ACT.Copy, scale=-1.0)
@@ -108,34 +111,49 @@ def tile_attend_gat_pl_lse_c_kernel(
             nc.vector.tensor_copy(c_grouped[:, :, l], pool[l][:].indirect(offsets[:]))
         c_mx = quantize("c", c_grouped[:].rearrange("p n l -> p (n l)"), E4)
 
-        q_mx = quantize("q", deal("q_grouped", q_raw, [("vector", 0, 88), ("scalar", 88, P)]), E4)
         a_banks = [psum.tile([P, N], F32, name="bank%d" % r) for r in range(LANES)]
         p_sb = keep.tile([P, LANES, N], F32, name="p_sb")
-        for r in range(LANES):
-            product(a_banks[r], q_mx, r, c_mx, True, True)
+        q_grouped = [grouped_tile("q_grouped%d" % h, 256) for h in range(2)]
+        deal("vector", q_grouped[0][:], q_raw, 0)
+        deal("scalar", q_grouped[1][:], q_raw, 1)
+        for h in range(2):
+            q_mx = quantize("q%d" % h, q_grouped[h][:], E4)
+            for j in range(2):
+                product(a_banks[2 * h + j], q_mx, j, c_mx, True, True)
         for r in range(LANES):
             nc.scalar.activation(p_sb[:, r, :], a_banks[r][:], ACT.Exp, bias=neg_lse[:, r : r + 1], scale=1.0)
 
-        do_mx = quantize("do", deal("do_grouped", do_raw, [("vector", 0, P)]), E5)
-        dp_banks = [psum.tile([P, N], F32, name="bank%d" % (LANES + r)) for r in range(LANES)]
-        for r in range(LANES):
-            product(dp_banks[r], do_mx, r, c_mx, True, True)
-
         pw_sb = keep.tile([P, LANES, N], F32, name="pw_sb")
         ds_sb = keep.tile([P, LANES, N], F32, name="ds_sb")
-        for r in range(LANES):
+
+        def gate(r):
             nc.vector.tensor_scalar(pw_sb[:, r, :], p_sb[:, r, :], rw_sb[:, r : r + 1], None, ALU.mult)
-        dom_grouped = deal("dom_grouped", dom_raw, [("scalar", 0, P)])
+
+        dp_banks = [psum.tile([P, N], F32, name="bank%d" % (LANES + r)) for r in range(LANES)]
+        do_grouped = [grouped_tile("do_grouped%d" % h, 256) for h in range(2)]
+        for h in range(2):
+            deal("vector", do_grouped[h][:], do_raw, h)
+        for h in range(2):
+            do_mx = quantize("do%d" % h, do_grouped[h][:], E5)
+            for j in range(2):
+                product(dp_banks[2 * h + j], do_mx, j, c_mx, True, True)
+        for r in range(LANES):
+            gate(r)
+        dom_grouped = grouped_tile("dom_grouped", 512)
+        qm_grouped = grouped_tile("qm_grouped", 512)
+        for h in range(2):
+            deal("scalar", dom_grouped[:, 1024 * h : 1024 * (h + 1)], dom_raw, h)
         for r in range(LANES):
             nc.vector.scalar_tensor_tensor(
                 ds_sb[:, r, :], dp_banks[r][:], delta_sb[:, r : r + 1], pw_sb[:, r, :], ALU.subtract, ALU.mult
             )
+        for h in range(2):
+            deal("scalar", qm_grouped[:, 1024 * h : 1024 * (h + 1)], qm_raw, h)
         pw_grouped = weave("pw_grouped", pw_sb[:], [("vector", 0, P)])
-        dom_mx = quantize("dom", dom_grouped, E5)
-        qm_grouped = deal("qm_grouped", qm_raw, [("scalar", 0, P)])
+        dom_mx = quantize("dom", dom_grouped[:], E5)
         pw_mx = quantize("pw", pw_grouped, E4)
-        ds_grouped = weave("ds_grouped", ds_sb[:], [("vector", 0, 64), ("scalar", 64, P)])
-        qm_mx = quantize("qm", qm_grouped, E4)
+        ds_grouped = weave("ds_grouped", ds_sb[:], [("vector", 0, 24), ("scalar", 24, P)])
+        qm_mx = quantize("qm", qm_grouped[:], E4)
         ds_mx = quantize("ds", ds_grouped, E5)
 
         g_banks = [psum.tile([P, N], F32, name="bank%d" % j) for j in range(LANES)]
@@ -147,7 +165,7 @@ def tile_attend_gat_pl_lse_c_kernel(
         out_planes = out_0.rearrange("(p l) t -> l p t", l=LANES)
         for j in range(LANES):
             g_sb = keep.tile([P, N], F32, name="g_sb%d" % j)
-            if j % 2 == 0:
+            if j % 2 == 1:
                 nc.scalar.copy(g_sb[:], g_banks[j][:])
                 for h in range(2):
                     nc.scalar.activation(
@@ -167,14 +185,25 @@ def tile_attend_gat_pl_lse_c_kernel(
         for u in range(chunks):
             cols = slice(CHUNK * u, CHUNK * (u + 1))
             for j in range(LANES):
-                copy("scalar" if j < 2 else "vector", rounded[u][:, j, :], windows[j][:, cols])
+                copy("scalar" if j % 2 == 1 else "vector", rounded[u][:, j, :], windows[j][:, cols])
+        shares = [[("vector", 0, P)], [("vector", 0, P)], [("scalar", 0, P)], [("vector", 0, 80), ("scalar", 80, P)]]
+        y_grouped = [None] * chunks
+
+        def emit(u, c0, c1):
+            y_codes = keep.tile([P, c1 - c0], U32, name="y_codes%d_%d" % (u, c0), align_bytes=64)
+            nc.vector.quantize_mx(
+                out=y_codes[:].bitcast(E4),
+                scales=y_scales[LANES * u :, c0:c1],
+                in_=y_grouped[u][:, LANES * c0 : LANES * c1],
+            )
+            nc.sync.dma_start(words[:, CHUNK * u + c0 : CHUNK * u + c1], y_codes[:].bitcast(I32))
+
         for u in range(chunks):
-            cols = slice(CHUNK * u, CHUNK * (u + 1))
-            shares = [[("vector", 0, P)], [("vector", 0, P)], [("vector", 0, 80), ("scalar", 80, P)], [("scalar", 0, P)]][u]
-            y_grouped = weave("y_grouped%d" % u, rounded[u][:], shares)
-            y_codes = keep.tile([P, CHUNK], U32, name="y_codes%d" % u, align_bytes=64)
-            nc.vector.quantize_mx(out=y_codes[:].bitcast(E4), scales=y_scales[LANES * u :, :], in_=y_grouped)
-            nc.sync.dma_start(words[:, cols], y_codes[:].bitcast(I32))
+            y_grouped[u] = weave("y_grouped%d" % u, rounded[u][:], shares[u])
+            if 0 < u < chunks - 1:
+                emit(u - 1, 0, CHUNK)
+        emit(chunks - 2, 0, CHUNK)
+        emit(chunks - 1, 0, CHUNK)
         scale_rows = out_2[0].bitcast(I32).rearrange("f (u c) -> u f c", u=chunks)
         for quad in range(4):
             queue = nc.sync if quad % 2 == 0 else nc.scalar

@@ -97,19 +97,19 @@ def tile_attend_gat_pl_lse_c_kernel(
         qm_raw = load_rows("qm_raw", qm)
 
         windows = [keep.tile([P, T], F32, name="window%d" % j) for j in range(LANES)]
-        for j in range(2):
+        for j in range(LANES):
             nc.vector.memset(windows[j][:], 0.0)
-        for j in range(2, LANES):
-            for h in range(2):
-                nc.gpsimd.memset(windows[j][:, h * T // 2 : (h + 1) * T // 2], 0.0)
 
         neg_lse = keep.tile([P, LANES], F32, name="neg_lse")
         nc.scalar.activation(neg_lse[:], lse_sb[:], ACT.Copy, scale=-1.0)
 
-        c_grouped = keep.tile([P, N, LANES], BF16, name="c_grouped", align_bytes=64)
-        for l in range(LANES):
-            nc.vector.tensor_copy(c_grouped[:, :, l], pool[l][:].indirect(offsets[:]))
-        c_mx = quantize("c", c_grouped[:].rearrange("p n l -> p (n l)"), E4)
+        c_picked = keep.tile([P, LANES, N], BF16, name="c_picked")
+        for l in range(LANES - 1):
+            nc.scalar.activation(c_picked[:, l, :], pool[l][:].indirect(offsets[:]), ACT.Copy)
+        last = LANES - 1
+        nc.vector.tensor_copy(c_picked[:, last, :320], pool[last][:].indirect(offsets[:, :20]))
+        nc.scalar.activation(c_picked[:, last, 320:], pool[last][:].indirect(offsets[:, 20:]), ACT.Copy)
+        c_mx = quantize("c", weave("c_grouped", c_picked[:], [("vector", 0, 84), ("scalar", 84, P)]), E4)
 
         a_banks = [psum.tile([P, N], F32, name="bank%d" % r) for r in range(LANES)]
         p_sb = keep.tile([P, LANES, N], F32, name="p_sb")
@@ -139,44 +139,59 @@ def tile_attend_gat_pl_lse_c_kernel(
                 product(dp_banks[2 * h + j], do_mx, j, c_mx, True, True)
         for r in range(LANES):
             gate(r)
-        dom_grouped = grouped_tile("dom_grouped", 512)
-        qm_grouped = grouped_tile("qm_grouped", 512)
-        for h in range(2):
-            deal("scalar", dom_grouped[:, 1024 * h : 1024 * (h + 1)], dom_raw, h)
+        dom_grouped = [grouped_tile("dom_grouped%d" % h, 256) for h in range(2)]
+        qm_grouped = [grouped_tile("qm_grouped%d" % h, 256) for h in range(2)]
+        deal("scalar", dom_grouped[0][:], dom_raw, 0)
         for r in range(LANES):
             nc.vector.scalar_tensor_tensor(
                 ds_sb[:, r, :], dp_banks[r][:], delta_sb[:, r : r + 1], pw_sb[:, r, :], ALU.subtract, ALU.mult
             )
-        for h in range(2):
-            deal("scalar", qm_grouped[:, 1024 * h : 1024 * (h + 1)], qm_raw, h)
-        pw_grouped = weave("pw_grouped", pw_sb[:], [("vector", 0, P)])
-        dom_mx = quantize("dom", dom_grouped[:], E5)
+        pw_grouped = weave("pw_grouped", pw_sb[:], [("vector", 0, 88), ("scalar", 88, P)])
+        deal("scalar", qm_grouped[0][:], qm_raw, 0)
+        dom_mx = [quantize("dom0", dom_grouped[0][:], E5)]
         pw_mx = quantize("pw", pw_grouped, E4)
-        ds_grouped = weave("ds_grouped", ds_sb[:], [("vector", 0, 24), ("scalar", 24, P)])
-        qm_mx = quantize("qm", qm_grouped[:], E4)
+        ds_grouped = weave("ds_grouped", ds_sb[:], [("vector", 0, 44), ("scalar", 44, P)])
+        qm_mx = [quantize("qm0", qm_grouped[0][:], E4)]
         ds_mx = quantize("ds", ds_grouped, E5)
+        deal("scalar", qm_grouped[1][:], qm_raw, 1)
+        deal("vector", dom_grouped[1][:], dom_raw, 1)
 
         g_banks = [psum.tile([P, N], F32, name="bank%d" % j) for j in range(LANES)]
-        for j in range(LANES):
-            product(g_banks[j], dom_mx, j, pw_mx, True, False)
-        for j in range(LANES):
-            product(g_banks[j], qm_mx, j, ds_mx, False, True)
-
+        g_sb = [keep.tile([P, N], F32, name="g_sb%d" % j) for j in range(LANES)]
         out_planes = out_0.rearrange("(p l) t -> l p t", l=LANES)
-        for j in range(LANES):
-            g_sb = keep.tile([P, N], F32, name="g_sb%d" % j)
-            if j % 2 == 1:
-                nc.scalar.copy(g_sb[:], g_banks[j][:])
+
+        def gradients(h):
+            for j in range(2):
+                product(g_banks[2 * h + j], dom_mx[h], j, pw_mx, True, False)
+            for j in range(2):
+                product(g_banks[2 * h + j], qm_mx[h], j, ds_mx, False, True)
+
+        def unload(j):
+            copy("scalar" if j % 2 else "vector", g_sb[j][:], g_banks[j][:])
+
+        def scatter(j):
+            if j % 2:
                 for h in range(2):
                     nc.scalar.activation(
                         windows[j][:].indirect(offsets[:, 16 * h : 16 * (h + 1)]),
-                        g_sb[:, HALF * h : HALF * (h + 1)],
+                        g_sb[j][:, HALF * h : HALF * (h + 1)],
                         ACT.Copy,
                     )
             else:
-                nc.vector.tensor_copy(g_sb[:], g_banks[j][:])
-                nc.vector.tensor_copy(windows[j][:].indirect(offsets[:]), g_sb[:])
+                nc.vector.tensor_copy(windows[j][:].indirect(offsets[:]), g_sb[j][:])
             nc.sync.dma_start(out_planes[j], windows[j][:])
+
+        gradients(0)
+        unload(0)
+        dom_mx.append(quantize("dom1", dom_grouped[1][:], E5))
+        qm_mx.append(quantize("qm1", qm_grouped[1][:], E4))
+        gradients(1)
+        unload(1)
+        scatter(0)
+        scatter(1)
+        for j in range(2, LANES):
+            unload(j)
+            scatter(j)
 
         chunks = T // CHUNK
         words = out_1.rearrange("o p t b -> p (o t b)").bitcast(I32)

@@ -3,7 +3,7 @@ from contextlib import ExitStack
 import concourse.mybir as mybir
 
 N, T, D, R = 512, 2048, 512, 512
-FLOPS = 4 * 2 * 512 * 512 * 512
+FLOPS = 4 * 2 * R * D * N
 
 F32 = mybir.dt.float32
 BF16 = mybir.dt.bfloat16
@@ -18,8 +18,19 @@ ACT = mybir.ActivationFunctionType
 
 P = 128
 LANES = 4
-CHUNK = 512
+LAST = LANES - 1
+RUN = 4
+PER_COLUMN = 16
 HALF = N // 2
+CHUNK = 512
+CHUNKS = T // CHUNK
+QUADRANT = 32
+
+VECTOR, SCALAR, GPSIMD = "vector", "scalar", "gpsimd"
+
+LAST_GATHER_SPLIT = 320
+LATENT_WEAVE_SPLIT = 336
+LAST_CHUNK_SPLIT = 128
 
 
 def tile_attend_gat_pl_lse_c_kernel(
@@ -31,42 +42,50 @@ def tile_attend_gat_pl_lse_c_kernel(
         psum = ctx.enter_context(tc.psum_pool(name="psum", bufs=1))
 
         def copy(engine, out, in_):
-            if engine == "scalar":
+            if engine == SCALAR:
                 nc.scalar.copy(out, in_)
+            elif engine == GPSIMD:
+                nc.gpsimd.tensor_scalar(out, in_, 1.0, 0.0, ALU.mult, ALU.add)
             else:
                 nc.vector.tensor_copy(out, in_)
 
-        def load_rows(name, src):
-            raw = keep.tile([P, LANES, 512], F32, name=name)
+        def load_planes(name, src):
+            raw = keep.tile([P, LANES, src.shape[2]], F32, name=name)
             nc.sync.dma_start(raw[:], src[0].rearrange("(p l) c -> p l c", l=LANES))
             return raw
 
-        def load_column(name, src):
-            col = keep.tile([P, LANES], F32, name=name)
-            nc.scalar.dma_start(col[:], src[0].rearrange("(p l) o -> p (l o)", l=LANES))
-            return col
+        def load_per_query(name, src):
+            numbers = keep.tile([P, LANES], F32, name=name)
+            nc.sync.dma_start(numbers[:], src[0].rearrange("(p l) o -> p (l o)", l=LANES))
+            return numbers
 
-        def deal(engine, dst, raw, half):
-            src = raw[:].rearrange("p l (m h j) -> p h m l j", h=2, j=2)[:, half]
-            copy(engine, dst.rearrange("p (j m l) -> p m l j", j=2, l=LANES), src)
+        def pair_tiles(name):
+            return [
+                keep.tile([P, 2 * P * LANES], BF16, name="%s%d" % (name, pair), align_bytes=64) for pair in range(2)
+            ]
 
-        def grouped_tile(name, words):
-            return keep.tile([P, words * LANES], BF16, name=name, align_bytes=64)
+        def deal(engine, dealt, raw, pair, places=slice(0, P)):
+            src = raw[:].rearrange("p l (m h j) -> p h m l j", h=2, j=2)[:, pair]
+            dst = dealt[pair][:].rearrange("p (j m l) -> p m l j", j=2, l=LANES)
+            copy(engine, dst[:, places], src[:, places])
 
         def weave(name, planes, shares):
-            width = planes.shape[2]
-            grouped = keep.tile([P, width, LANES], BF16, name=name, align_bytes=64)
-            dst = grouped[:].rearrange("p (c i) l -> p c l i", i=4)
-            src = planes.rearrange("p l (c i) -> p c l i", i=4)
-            for engine, c0, c1 in shares:
-                copy(engine, dst[:, c0:c1], src[:, c0:c1])
-            return grouped[:].rearrange("p n l -> p (n l)")
+            woven = keep.tile([P, planes.shape[2], LANES], BF16, name=name, align_bytes=64)
+            for engine, first, end in shares:
+                if engine == GPSIMD:
+                    copy(engine, woven[:, first:end, :], planes.rearrange("p l n -> p n l")[:, first:end, :])
+                else:
+                    runs = slice(first // RUN, end // RUN)
+                    dst = woven[:].rearrange("p (c i) l -> p c l i", i=RUN)
+                    src = planes.rearrange("p l (c i) -> p c l i", i=RUN)
+                    copy(engine, dst[:, runs], src[:, runs])
+            return woven[:].rearrange("p n l -> p (n l)")
 
-        def quantize(name, grouped, fmt):
-            words = grouped.shape[1] // LANES
-            codes = keep.tile([P, words], U32, name=name + "_codes", align_bytes=64)
-            scales = keep.tile([P, words], U8, name=name + "_scales", align_bytes=64)
-            nc.vector.quantize_mx(out=codes[:].bitcast(fmt), scales=scales[:], in_=grouped)
+        def quantize(name, woven, fmt):
+            columns = woven.shape[1] // LANES
+            codes = keep.tile([P, columns], U32, name=name + "_codes", align_bytes=64)
+            scales = keep.tile([P, columns], U8, name=name + "_scales", align_bytes=64)
+            nc.vector.quantize_mx(out=codes[:].bitcast(fmt), scales=scales[:], in_=woven)
             return codes, scales, fmt
 
         def product(bank, stationary, j, moving, start, stop):
@@ -81,148 +100,170 @@ def tile_attend_gat_pl_lse_c_kernel(
                 stop=stop,
             )
 
-        offsets = keep.tile([P, N // 16], U16, name="offsets")
+        offsets = keep.tile([P, N // PER_COLUMN], U16, name="offsets")
         c_planes = cT.rearrange("(p l) t -> l p t", l=LANES)
-        pool = [keep.tile([P, T], F32, name="pool%d" % l) for l in range(LANES)]
-        nc.sync.dma_start(pool[0][:], c_planes[0])
+        latents = [keep.tile([P, T], F32, name="latents%d" % l) for l in range(LANES)]
+        nc.sync.dma_start(latents[0][:], c_planes[0])
         nc.sync.dma_start(offsets[:], offs)
         for l in range(1, LANES):
-            nc.sync.dma_start(pool[l][:], c_planes[l])
-        lse_sb = load_column("lse_sb", lse)
-        delta_sb = load_column("delta_sb", delta)
-        rw_sb = load_column("rw_sb", rw)
-        q_raw = load_rows("q_raw", qT)
-        do_raw = load_rows("do_raw", doT)
-        dom_raw = load_rows("dom_raw", dom)
-        qm_raw = load_rows("qm_raw", qm)
+            nc.sync.dma_start(latents[l][:], c_planes[l])
+        q_raw = load_planes("q_raw", qT)
+        lse_sb = load_per_query("lse_sb", lse)
+        do_raw = load_planes("do_raw", doT)
+        rw_sb = load_per_query("rw_sb", rw)
+        delta_sb = load_per_query("delta_sb", delta)
+        dom_raw = load_planes("dom_raw", dom)
+        qm_raw = load_planes("qm_raw", qm)
+
+        def listed(tile, first, end):
+            return tile[:].indirect(offsets[:, first // PER_COLUMN : end // PER_COLUMN])
 
         windows = [keep.tile([P, T], F32, name="window%d" % j) for j in range(LANES)]
         for j in range(LANES):
             nc.vector.memset(windows[j][:], 0.0)
 
-        neg_lse = keep.tile([P, LANES], F32, name="neg_lse")
-        nc.scalar.activation(neg_lse[:], lse_sb[:], ACT.Copy, scale=-1.0)
-
         c_picked = keep.tile([P, LANES, N], BF16, name="c_picked")
-        for l in range(LANES - 1):
-            nc.scalar.activation(c_picked[:, l, :], pool[l][:].indirect(offsets[:]), ACT.Copy)
-        last = LANES - 1
-        nc.vector.tensor_copy(c_picked[:, last, :320], pool[last][:].indirect(offsets[:, :20]))
-        nc.scalar.activation(c_picked[:, last, 320:], pool[last][:].indirect(offsets[:, 20:]), ACT.Copy)
-        c_mx = quantize("c", weave("c_grouped", c_picked[:], [("vector", 0, 84), ("scalar", 84, P)]), E4)
+        for l in range(LAST):
+            nc.scalar.activation(c_picked[:, l, :], listed(latents[l], 0, N), ACT.Copy)
+        nc.vector.tensor_copy(c_picked[:, LAST, :LAST_GATHER_SPLIT], listed(latents[LAST], 0, LAST_GATHER_SPLIT))
+        nc.scalar.activation(
+            c_picked[:, LAST, LAST_GATHER_SPLIT:], listed(latents[LAST], LAST_GATHER_SPLIT, N), ACT.Copy
+        )
+        c_woven = weave("c_woven", c_picked[:], [(VECTOR, 0, LATENT_WEAVE_SPLIT), (SCALAR, LATENT_WEAVE_SPLIT, N)])
+        c_mx = quantize("c", c_woven, E4)
 
         a_banks = [psum.tile([P, N], F32, name="bank%d" % r) for r in range(LANES)]
         p_sb = keep.tile([P, LANES, N], F32, name="p_sb")
-        q_grouped = [grouped_tile("q_grouped%d" % h, 256) for h in range(2)]
-        deal("vector", q_grouped[0][:], q_raw, 0)
-        deal("scalar", q_grouped[1][:], q_raw, 1)
-        for h in range(2):
-            q_mx = quantize("q%d" % h, q_grouped[h][:], E4)
+        q_dealt = pair_tiles("q_dealt")
+        deal(SCALAR, q_dealt, q_raw, 0, slice(0, P // 2))
+        deal(VECTOR, q_dealt, q_raw, 0, slice(P // 2, P))
+        deal(SCALAR, q_dealt, q_raw, 1)
+        neg_lse = keep.tile([P, LANES], F32, name="neg_lse")
+        nc.scalar.activation(neg_lse[:], lse_sb[:], ACT.Copy, scale=-1.0)
+        for pair in range(2):
+            q_mx = quantize("q%d" % pair, q_dealt[pair][:], E4)
             for j in range(2):
-                product(a_banks[2 * h + j], q_mx, j, c_mx, True, True)
+                product(a_banks[2 * pair + j], q_mx, j, c_mx, True, True)
         for r in range(LANES):
             nc.scalar.activation(p_sb[:, r, :], a_banks[r][:], ACT.Exp, bias=neg_lse[:, r : r + 1], scale=1.0)
 
         pw_sb = keep.tile([P, LANES, N], F32, name="pw_sb")
         ds_sb = keep.tile([P, LANES, N], F32, name="ds_sb")
-
-        def gate(r):
+        dp_banks = [psum.tile([P, N], F32, name="bank%d" % (LANES + r)) for r in range(LANES)]
+        do_dealt = pair_tiles("do_dealt")
+        for pair in range(2):
+            deal(VECTOR, do_dealt, do_raw, pair)
+        for pair in range(2):
+            do_mx = quantize("do%d" % pair, do_dealt[pair][:], E5)
+            for j in range(2):
+                product(dp_banks[2 * pair + j], do_mx, j, c_mx, True, True)
+        for r in range(LANES):
             nc.vector.tensor_scalar(pw_sb[:, r, :], p_sb[:, r, :], rw_sb[:, r : r + 1], None, ALU.mult)
 
-        dp_banks = [psum.tile([P, N], F32, name="bank%d" % (LANES + r)) for r in range(LANES)]
-        do_grouped = [grouped_tile("do_grouped%d" % h, 256) for h in range(2)]
-        for h in range(2):
-            deal("vector", do_grouped[h][:], do_raw, h)
-        for h in range(2):
-            do_mx = quantize("do%d" % h, do_grouped[h][:], E5)
-            for j in range(2):
-                product(dp_banks[2 * h + j], do_mx, j, c_mx, True, True)
-        for r in range(LANES):
-            gate(r)
-        dom_grouped = [grouped_tile("dom_grouped%d" % h, 256) for h in range(2)]
-        qm_grouped = [grouped_tile("qm_grouped%d" % h, 256) for h in range(2)]
-        deal("scalar", dom_grouped[0][:], dom_raw, 0)
+        dom_dealt = pair_tiles("dom_dealt")
+        qm_dealt = pair_tiles("qm_dealt")
+        halves = [slice(HALF * s, HALF * (s + 1)) for s in range(2)]
+        pw_woven = [weave("pw_woven0", pw_sb[:, :, halves[0]], [(GPSIMD, 0, HALF)])]
+        deal(SCALAR, dom_dealt, dom_raw, 0)
         for r in range(LANES):
             nc.vector.scalar_tensor_tensor(
                 ds_sb[:, r, :], dp_banks[r][:], delta_sb[:, r : r + 1], pw_sb[:, r, :], ALU.subtract, ALU.mult
             )
-        pw_grouped = weave("pw_grouped", pw_sb[:], [("vector", 0, 88), ("scalar", 88, P)])
-        deal("scalar", qm_grouped[0][:], qm_raw, 0)
-        dom_mx = [quantize("dom0", dom_grouped[0][:], E5)]
-        pw_mx = quantize("pw", pw_grouped, E4)
-        ds_grouped = weave("ds_grouped", ds_sb[:], [("vector", 0, 44), ("scalar", 44, P)])
-        qm_mx = [quantize("qm0", qm_grouped[0][:], E4)]
-        ds_mx = quantize("ds", ds_grouped, E5)
-        deal("scalar", qm_grouped[1][:], qm_raw, 1)
-        deal("vector", dom_grouped[1][:], dom_raw, 1)
+        deal(SCALAR, dom_dealt, dom_raw, 1)
+        deal(SCALAR, qm_dealt, qm_raw, 0)
+        deal(SCALAR, qm_dealt, qm_raw, 1)
 
-        g_banks = [psum.tile([P, N], F32, name="bank%d" % j) for j in range(LANES)]
-        g_sb = [keep.tile([P, N], F32, name="g_sb%d" % j) for j in range(LANES)]
+        dom_mx, qm_mx, pw_mx, ds_mx = [], [], [], []
+        g_banks, g_sb = {}, {}
         out_planes = out_0.rearrange("(p l) t -> l p t", l=LANES)
 
-        def gradients(h):
+        def value_pass(pair, s):
             for j in range(2):
-                product(g_banks[2 * h + j], dom_mx[h], j, pw_mx, True, False)
+                bank = psum.tile([P, HALF], F32, name="bank%d" % (LANES * s + 2 * pair + j))
+                g_banks[2 * pair + j, s] = bank
+                product(bank, dom_mx[pair], j, pw_mx[s], True, False)
+
+        def key_pass(pair, s):
             for j in range(2):
-                product(g_banks[2 * h + j], qm_mx[h], j, ds_mx, False, True)
+                product(g_banks[2 * pair + j, s], qm_mx[pair], j, ds_mx[s], False, True)
 
-        def unload(j):
-            copy("scalar" if j % 2 else "vector", g_sb[j][:], g_banks[j][:])
+        def scatter_engine(j, s):
+            return VECTOR if s == 1 and j < LAST else SCALAR
 
-        def scatter(j):
-            if j % 2:
-                for h in range(2):
-                    nc.scalar.activation(
-                        windows[j][:].indirect(offsets[:, 16 * h : 16 * (h + 1)]),
-                        g_sb[j][:, HALF * h : HALF * (h + 1)],
-                        ACT.Copy,
-                    )
+        def unload(j, s):
+            g_sb[j, s] = keep.tile([P, HALF], F32, name="g_sb%d_%d" % (j, s))
+            copy(scatter_engine(j, s), g_sb[j, s][:], g_banks[j, s][:])
+
+        def scatter(j, s):
+            places = listed(windows[j], HALF * s, HALF * (s + 1))
+            if scatter_engine(j, s) == VECTOR:
+                nc.vector.tensor_copy(places, g_sb[j, s][:])
             else:
-                nc.vector.tensor_copy(windows[j][:].indirect(offsets[:]), g_sb[j][:])
-            nc.sync.dma_start(out_planes[j], windows[j][:])
+                nc.scalar.activation(places, g_sb[j, s][:], ACT.Copy)
+            if s == 1:
+                nc.sync.dma_start(out_planes[j], windows[j][:])
 
-        gradients(0)
-        unload(0)
-        dom_mx.append(quantize("dom1", dom_grouped[1][:], E5))
-        qm_mx.append(quantize("qm1", qm_grouped[1][:], E4))
-        gradients(1)
-        unload(1)
-        scatter(0)
-        scatter(1)
-        for j in range(2, LANES):
-            unload(j)
-            scatter(j)
+        ds_woven = [weave("ds_woven0", ds_sb[:, :, halves[0]], [(VECTOR, 0, HALF)])]
+        dom_mx.append(quantize("dom0", dom_dealt[0][:], E5))
+        pw_mx.append(quantize("pw0", pw_woven[0], E4))
+        value_pass(0, 0)
+        qm_mx.append(quantize("qm0", qm_dealt[0][:], E4))
+        ds_mx.append(quantize("ds0", ds_woven[0], E5))
+        key_pass(0, 0)
+        pw_woven.append(weave("pw_woven1", pw_sb[:, :, halves[1]], [(VECTOR, 0, HALF)]))
+        ds_woven.append(weave("ds_woven1", ds_sb[:, :, halves[1]], [(VECTOR, 0, HALF)]))
+        pw_mx.append(quantize("pw1", pw_woven[1], E4))
+        value_pass(0, 1)
+        ds_mx.append(quantize("ds1", ds_woven[1], E5))
+        key_pass(0, 1)
+        dom_mx.append(quantize("dom1", dom_dealt[1][:], E5))
+        unload(0, 0)
+        unload(0, 1)
+        qm_mx.append(quantize("qm1", qm_dealt[1][:], E4))
+        for s in range(2):
+            value_pass(1, s)
+            key_pass(1, s)
+        for j in range(LANES):
+            for s in range(2):
+                if j > 0:
+                    unload(j, s)
+                scatter(j, s)
 
-        chunks = T // CHUNK
+        def rounding_engine(j, u):
+            if j == 0 or (j == 1 and u < CHUNKS // 2):
+                return GPSIMD
+            if j == LAST and u >= CHUNKS // 2:
+                return SCALAR
+            return VECTOR
+
         words = out_1.rearrange("o p t b -> p (o t b)").bitcast(I32)
         y_scales = keep.tile([P, CHUNK], U8, name="y_scales", align_bytes=64)
-        rounded = [keep.tile([P, LANES, CHUNK], BF16, name="rounded%d" % u) for u in range(chunks)]
-        for u in range(chunks):
-            cols = slice(CHUNK * u, CHUNK * (u + 1))
-            for j in range(LANES):
-                copy("scalar" if j % 2 == 1 else "vector", rounded[u][:, j, :], windows[j][:, cols])
-        shares = [[("vector", 0, P)], [("vector", 0, P)], [("scalar", 0, P)], [("vector", 0, 80), ("scalar", 80, P)]]
-        y_grouped = [None] * chunks
+        rounded = [keep.tile([P, LANES, CHUNK], BF16, name="rounded%d" % u) for u in range(CHUNKS)]
+        for j in range(LANES):
+            for u in range(CHUNKS):
+                copy(rounding_engine(j, u), rounded[u][:, j, :], windows[j][:, CHUNK * u : CHUNK * (u + 1)])
 
-        def emit(u, c0, c1):
-            y_codes = keep.tile([P, c1 - c0], U32, name="y_codes%d_%d" % (u, c0), align_bytes=64)
-            nc.vector.quantize_mx(
-                out=y_codes[:].bitcast(E4),
-                scales=y_scales[LANES * u :, c0:c1],
-                in_=y_grouped[u][:, LANES * c0 : LANES * c1],
-            )
-            nc.sync.dma_start(words[:, CHUNK * u + c0 : CHUNK * u + c1], y_codes[:].bitcast(I32))
+        def emit(u, woven):
+            y_codes = keep.tile([P, CHUNK], U32, name="y_codes%d" % u, align_bytes=64)
+            nc.vector.quantize_mx(out=y_codes[:].bitcast(E4), scales=y_scales[LANES * u :, :], in_=woven)
+            nc.sync.dma_start(words[:, CHUNK * u : CHUNK * (u + 1)], y_codes[:].bitcast(I32))
 
-        for u in range(chunks):
-            y_grouped[u] = weave("y_grouped%d" % u, rounded[u][:], shares[u])
-            if 0 < u < chunks - 1:
-                emit(u - 1, 0, CHUNK)
-        emit(chunks - 2, 0, CHUNK)
-        emit(chunks - 1, 0, CHUNK)
-        scale_rows = out_2[0].bitcast(I32).rearrange("f (u c) -> u f c", u=chunks)
-        for quad in range(4):
+        y_shares = [
+            [(VECTOR, 0, CHUNK)],
+            [(VECTOR, 0, CHUNK)],
+            [(SCALAR, 0, CHUNK)],
+            [(VECTOR, 0, LAST_CHUNK_SPLIT), (SCALAR, LAST_CHUNK_SPLIT, CHUNK)],
+        ]
+        y_woven = [weave("y_woven0", rounded[0][:], y_shares[0])]
+        for u in range(1, CHUNKS):
+            y_woven.append(weave("y_woven%d" % u, rounded[u][:], y_shares[u]))
+            emit(u - 1, y_woven[u - 1])
+        emit(CHUNKS - 1, y_woven[CHUNKS - 1])
+
+        scale_rows = out_2[0].bitcast(I32).rearrange("f (u c) -> u f c", u=CHUNKS)
+        for quad in range(P // QUADRANT):
             queue = nc.sync if quad % 2 == 0 else nc.scalar
             queue.dma_start(
-                scale_rows[:, 4 * quad : 4 * quad + 4, :],
-                y_scales[32 * quad : 32 * quad + 16, :].bitcast(I32),
+                scale_rows[:, LANES * quad : LANES * (quad + 1), :],
+                y_scales[QUADRANT * quad : QUADRANT * quad + LANES * CHUNKS, :].bitcast(I32),
             )

from contextlib import ExitStack

import concourse.mybir as mybir

N, T, D, R = 512, 2048, 512, 512
FLOPS = 4 * 2 * R * D * N

F32 = mybir.dt.float32
BF16 = mybir.dt.bfloat16
I32 = mybir.dt.int32
U32 = mybir.dt.uint32
U16 = mybir.dt.uint16
U8 = mybir.dt.uint8
E4 = mybir.dt.float8_e4m3fn_x4
E5 = mybir.dt.float8_e5m2_x4
ALU = mybir.AluOpType
ACT = mybir.ActivationFunctionType

P = 128
LANES = 4
LAST = LANES - 1
RUN = 4
PER_COLUMN = 16
HALF = N // 2
CHUNK = 512
CHUNKS = T // CHUNK
QUADRANT = 32

VECTOR, SCALAR, GPSIMD = "vector", "scalar", "gpsimd"

LAST_GATHER_SPLIT = 320
LATENT_WEAVE_SPLIT = 336
LAST_CHUNK_SPLIT = 128


def tile_attend_gat_pl_lse_c_kernel(
    tc, qT, cT, doT, lse, delta, rw, qm, dom, offs, out_0, out_1, out_2
):
    nc = tc.nc
    with ExitStack() as ctx:
        keep = ctx.enter_context(tc.tile_pool(name="keep", bufs=1))
        psum = ctx.enter_context(tc.psum_pool(name="psum", bufs=1))

        def copy(engine, out, in_):
            if engine == SCALAR:
                nc.scalar.copy(out, in_)
            elif engine == GPSIMD:
                nc.gpsimd.tensor_scalar(out, in_, 1.0, 0.0, ALU.mult, ALU.add)
            else:
                nc.vector.tensor_copy(out, in_)

        def load_planes(name, src):
            raw = keep.tile([P, LANES, src.shape[2]], F32, name=name)
            nc.sync.dma_start(raw[:], src[0].rearrange("(p l) c -> p l c", l=LANES))
            return raw

        def load_per_query(name, src):
            numbers = keep.tile([P, LANES], F32, name=name)
            nc.sync.dma_start(numbers[:], src[0].rearrange("(p l) o -> p (l o)", l=LANES))
            return numbers

        def pair_tiles(name):
            return [
                keep.tile([P, 2 * P * LANES], BF16, name="%s%d" % (name, pair), align_bytes=64) for pair in range(2)
            ]

        def deal(engine, dealt, raw, pair, places=slice(0, P)):
            src = raw[:].rearrange("p l (m h j) -> p h m l j", h=2, j=2)[:, pair]
            dst = dealt[pair][:].rearrange("p (j m l) -> p m l j", j=2, l=LANES)
            copy(engine, dst[:, places], src[:, places])

        def weave(name, planes, shares):
            woven = keep.tile([P, planes.shape[2], LANES], BF16, name=name, align_bytes=64)
            for engine, first, end in shares:
                if engine == GPSIMD:
                    copy(engine, woven[:, first:end, :], planes.rearrange("p l n -> p n l")[:, first:end, :])
                else:
                    runs = slice(first // RUN, end // RUN)
                    dst = woven[:].rearrange("p (c i) l -> p c l i", i=RUN)
                    src = planes.rearrange("p l (c i) -> p c l i", i=RUN)
                    copy(engine, dst[:, runs], src[:, runs])
            return woven[:].rearrange("p n l -> p (n l)")

        def quantize(name, woven, fmt):
            columns = woven.shape[1] // LANES
            codes = keep.tile([P, columns], U32, name=name + "_codes", align_bytes=64)
            scales = keep.tile([P, columns], U8, name=name + "_scales", align_bytes=64)
            nc.vector.quantize_mx(out=codes[:].bitcast(fmt), scales=scales[:], in_=woven)
            return codes, scales, fmt

        def product(bank, stationary, j, moving, start, stop):
            cols = slice(P * j, P * (j + 1))
            nc.tensor.matmul_mx(
                out=bank[:],
                lhsT=stationary[0][:, cols].bitcast(stationary[2]),
                lhsT_scale=stationary[1][:, cols],
                rhs=moving[0][:].bitcast(moving[2]),
                rhs_scale=moving[1][:],
                start=start,
                stop=stop,
            )

        offsets = keep.tile([P, N // PER_COLUMN], U16, name="offsets")
        c_planes = cT.rearrange("(p l) t -> l p t", l=LANES)
        latents = [keep.tile([P, T], F32, name="latents%d" % l) for l in range(LANES)]
        nc.sync.dma_start(latents[0][:], c_planes[0])
        nc.sync.dma_start(offsets[:], offs)
        for l in range(1, LANES):
            nc.sync.dma_start(latents[l][:], c_planes[l])
        q_raw = load_planes("q_raw", qT)
        lse_sb = load_per_query("lse_sb", lse)
        do_raw = load_planes("do_raw", doT)
        rw_sb = load_per_query("rw_sb", rw)
        delta_sb = load_per_query("delta_sb", delta)
        dom_raw = load_planes("dom_raw", dom)
        qm_raw = load_planes("qm_raw", qm)

        def listed(tile, first, end):
            return tile[:].indirect(offsets[:, first // PER_COLUMN : end // PER_COLUMN])

        windows = [keep.tile([P, T], F32, name="window%d" % j) for j in range(LANES)]
        for j in range(LANES):
            nc.vector.memset(windows[j][:], 0.0)

        c_picked = keep.tile([P, LANES, N], BF16, name="c_picked")
        for l in range(LAST):
            nc.scalar.activation(c_picked[:, l, :], listed(latents[l], 0, N), ACT.Copy)
        nc.vector.tensor_copy(c_picked[:, LAST, :LAST_GATHER_SPLIT], listed(latents[LAST], 0, LAST_GATHER_SPLIT))
        nc.scalar.activation(
            c_picked[:, LAST, LAST_GATHER_SPLIT:], listed(latents[LAST], LAST_GATHER_SPLIT, N), ACT.Copy
        )
        c_woven = weave("c_woven", c_picked[:], [(VECTOR, 0, LATENT_WEAVE_SPLIT), (SCALAR, LATENT_WEAVE_SPLIT, N)])
        c_mx = quantize("c", c_woven, E4)

        a_banks = [psum.tile([P, N], F32, name="bank%d" % r) for r in range(LANES)]
        p_sb = keep.tile([P, LANES, N], F32, name="p_sb")
        q_dealt = pair_tiles("q_dealt")
        deal(SCALAR, q_dealt, q_raw, 0, slice(0, P // 2))
        deal(VECTOR, q_dealt, q_raw, 0, slice(P // 2, P))
        deal(SCALAR, q_dealt, q_raw, 1)
        neg_lse = keep.tile([P, LANES], F32, name="neg_lse")
        nc.scalar.activation(neg_lse[:], lse_sb[:], ACT.Copy, scale=-1.0)
        for pair in range(2):
            q_mx = quantize("q%d" % pair, q_dealt[pair][:], E4)
            for j in range(2):
                product(a_banks[2 * pair + j], q_mx, j, c_mx, True, True)
        for r in range(LANES):
            nc.scalar.activation(p_sb[:, r, :], a_banks[r][:], ACT.Exp, bias=neg_lse[:, r : r + 1], scale=1.0)

        pw_sb = keep.tile([P, LANES, N], F32, name="pw_sb")
        ds_sb = keep.tile([P, LANES, N], F32, name="ds_sb")
        dp_banks = [psum.tile([P, N], F32, name="bank%d" % (LANES + r)) for r in range(LANES)]
        do_dealt = pair_tiles("do_dealt")
        for pair in range(2):
            deal(VECTOR, do_dealt, do_raw, pair)
        for pair in range(2):
            do_mx = quantize("do%d" % pair, do_dealt[pair][:], E5)
            for j in range(2):
                product(dp_banks[2 * pair + j], do_mx, j, c_mx, True, True)
        for r in range(LANES):
            nc.vector.tensor_scalar(pw_sb[:, r, :], p_sb[:, r, :], rw_sb[:, r : r + 1], None, ALU.mult)

        dom_dealt = pair_tiles("dom_dealt")
        qm_dealt = pair_tiles("qm_dealt")
        halves = [slice(HALF * s, HALF * (s + 1)) for s in range(2)]
        pw_woven = [weave("pw_woven0", pw_sb[:, :, halves[0]], [(GPSIMD, 0, HALF)])]
        deal(SCALAR, dom_dealt, dom_raw, 0)
        for r in range(LANES):
            nc.vector.scalar_tensor_tensor(
                ds_sb[:, r, :], dp_banks[r][:], delta_sb[:, r : r + 1], pw_sb[:, r, :], ALU.subtract, ALU.mult
            )
        deal(SCALAR, dom_dealt, dom_raw, 1)
        deal(SCALAR, qm_dealt, qm_raw, 0)
        deal(SCALAR, qm_dealt, qm_raw, 1)

        dom_mx, qm_mx, pw_mx, ds_mx = [], [], [], []
        g_banks, g_sb = {}, {}
        out_planes = out_0.rearrange("(p l) t -> l p t", l=LANES)

        def value_pass(pair, s):
            for j in range(2):
                bank = psum.tile([P, HALF], F32, name="bank%d" % (LANES * s + 2 * pair + j))
                g_banks[2 * pair + j, s] = bank
                product(bank, dom_mx[pair], j, pw_mx[s], True, False)

        def key_pass(pair, s):
            for j in range(2):
                product(g_banks[2 * pair + j, s], qm_mx[pair], j, ds_mx[s], False, True)

        def scatter_engine(j, s):
            return VECTOR if s == 1 and j < LAST else SCALAR

        def unload(j, s):
            g_sb[j, s] = keep.tile([P, HALF], F32, name="g_sb%d_%d" % (j, s))
            copy(scatter_engine(j, s), g_sb[j, s][:], g_banks[j, s][:])

        def scatter(j, s):
            places = listed(windows[j], HALF * s, HALF * (s + 1))
            if scatter_engine(j, s) == VECTOR:
                nc.vector.tensor_copy(places, g_sb[j, s][:])
            else:
                nc.scalar.activation(places, g_sb[j, s][:], ACT.Copy)
            if s == 1:
                nc.sync.dma_start(out_planes[j], windows[j][:])

        ds_woven = [weave("ds_woven0", ds_sb[:, :, halves[0]], [(VECTOR, 0, HALF)])]
        dom_mx.append(quantize("dom0", dom_dealt[0][:], E5))
        pw_mx.append(quantize("pw0", pw_woven[0], E4))
        value_pass(0, 0)
        qm_mx.append(quantize("qm0", qm_dealt[0][:], E4))
        ds_mx.append(quantize("ds0", ds_woven[0], E5))
        key_pass(0, 0)
        pw_woven.append(weave("pw_woven1", pw_sb[:, :, halves[1]], [(VECTOR, 0, HALF)]))
        ds_woven.append(weave("ds_woven1", ds_sb[:, :, halves[1]], [(VECTOR, 0, HALF)]))
        pw_mx.append(quantize("pw1", pw_woven[1], E4))
        value_pass(0, 1)
        ds_mx.append(quantize("ds1", ds_woven[1], E5))
        key_pass(0, 1)
        dom_mx.append(quantize("dom1", dom_dealt[1][:], E5))
        unload(0, 0)
        unload(0, 1)
        qm_mx.append(quantize("qm1", qm_dealt[1][:], E4))
        for s in range(2):
            value_pass(1, s)
            key_pass(1, s)
        for j in range(LANES):
            for s in range(2):
                if j > 0:
                    unload(j, s)
                scatter(j, s)

        def rounding_engine(j, u):
            if j == 0 or (j == 1 and u < CHUNKS // 2):
                return GPSIMD
            if j == LAST and u >= CHUNKS // 2:
                return SCALAR
            return VECTOR

        words = out_1.rearrange("o p t b -> p (o t b)").bitcast(I32)
        y_scales = keep.tile([P, CHUNK], U8, name="y_scales", align_bytes=64)
        rounded = [keep.tile([P, LANES, CHUNK], BF16, name="rounded%d" % u) for u in range(CHUNKS)]
        for j in range(LANES):
            for u in range(CHUNKS):
                copy(rounding_engine(j, u), rounded[u][:, j, :], windows[j][:, CHUNK * u : CHUNK * (u + 1)])

        def emit(u, woven):
            y_codes = keep.tile([P, CHUNK], U32, name="y_codes%d" % u, align_bytes=64)
            nc.vector.quantize_mx(out=y_codes[:].bitcast(E4), scales=y_scales[LANES * u :, :], in_=woven)
            nc.sync.dma_start(words[:, CHUNK * u : CHUNK * (u + 1)], y_codes[:].bitcast(I32))

        y_shares = [
            [(VECTOR, 0, CHUNK)],
            [(VECTOR, 0, CHUNK)],
            [(SCALAR, 0, CHUNK)],
            [(VECTOR, 0, LAST_CHUNK_SPLIT), (SCALAR, LAST_CHUNK_SPLIT, CHUNK)],
        ]
        y_woven = [weave("y_woven0", rounded[0][:], y_shares[0])]
        for u in range(1, CHUNKS):
            y_woven.append(weave("y_woven%d" % u, rounded[u][:], y_shares[u]))
            emit(u - 1, y_woven[u - 1])
        emit(CHUNKS - 1, y_woven[CHUNKS - 1])

        scale_rows = out_2[0].bitcast(I32).rearrange("f (u c) -> u f c", u=CHUNKS)
        for quad in range(P // QUADRANT):
            queue = nc.sync if quad % 2 == 0 else nc.scalar
            queue.dma_start(
                scale_rows[:, LANES * quad : LANES * (quad + 1), :],
                y_scales[QUADRANT * quad : QUADRANT * quad + LANES * CHUNKS, :].bitcast(I32),
            )
